import numpy as np
import ml_dtypes


def mxq(x, axis, fmt="e4m3"):
    dtype, down = {"e4m3": (ml_dtypes.float8_e4m3fn, 7), "e5m2": (ml_dtypes.float8_e5m2, 14)}[fmt]
    v = np.moveaxis(np.asarray(x, np.float32).astype(ml_dtypes.bfloat16).astype(np.float64), axis, -1)
    blocks = v.reshape(v.shape[:-1] + (-1, 32))
    amax = np.abs(blocks).max(-1, keepdims=True)
    byte = np.maximum(np.where(amax > 0, np.frexp(amax)[1] - 1 + 127, 0) - down, 1)
    scale = np.exp2(byte - 127.0)
    codes = (blocks / scale).astype(np.float32).astype(dtype).astype(np.float64)
    return np.moveaxis((codes * scale).reshape(v.shape), -1, axis)


WIDE = False


def mx_kscale(k):
    if not WIDE:
        return np.ones(k)
    levels = np.array([10, -10, 5, -5, 0])
    if k % 512:
        return np.exp2(np.random.permutation(np.resize(levels, k // 32))).repeat(32)
    a = np.empty((k // 512, 16))
    for p in range(k // 512):
        a[p, :8] = np.random.permutation(np.resize(levels, 8))
        for g in range(8):
            far = levels[np.abs(levels - a[p, g]) >= 10]
            a[p, g + 8] = far[np.random.randint(len(far))]
    return np.exp2(a.ravel()).repeat(32)


def f64(x):
    return np.asarray(x).astype(np.float64)


def striped8(idx):
    return np.concatenate([v.reshape(-1, 16).T for v in idx]).astype(np.uint16)


def unstriped8(offs):
    return np.stack([offs[16 * g:16 * g + 16].T.reshape(-1) for g in range(8)]).astype(np.int64)


E2M1 = np.array([0.0, 0.5, 1.0, 1.5, 2.0, 3.0, 4.0, 6.0, -0.0, -0.5, -1.0, -1.5, -2.0, -3.0, -4.0, -6.0])


def pack_weight(w, fmt):
    k, n = w.shape
    w = f64(np.asarray(w, np.float32).astype(ml_dtypes.bfloat16)).reshape(k // 32, 32, n)
    amax = np.abs(w).max(1)
    if fmt == "e4m3":
        byte = np.frexp(amax)[1] - 1 + 127 - 7
    else:
        mant, ex = np.frexp(amax / 6.0)
        byte = np.where(mant > 0.5, ex, ex - 1) + 127
    byte = np.clip(np.where(amax > 0, byte, 1), 1, 254)
    scaled = (w * np.exp2(127.0 - byte)[:, None, :]).reshape(k, n).astype(np.float32)
    by_word = np.ascontiguousarray(scaled.reshape(k // 512, 128, 4, n).transpose(0, 1, 3, 2))
    if fmt == "e4m3":
        words = by_word.astype(ml_dtypes.float8_e4m3fn).view(np.uint8)
    else:
        c = by_word.astype(ml_dtypes.float4_e2m1fn).view(np.uint8) & 0xF
        words = (c[..., 0::2] | (c[..., 1::2] << 4)).reshape(k // 512, 128, 2 * n)
    return np.ascontiguousarray(words), np.ascontiguousarray(byte.astype(np.uint8).reshape(k // 512, 16, n))


def unpack_weight(words, scales, fmt):
    g, _, n = scales.shape
    words = np.ascontiguousarray(words).reshape(g, 128, n, -1)
    if fmt == "e4m3":
        vals = words.view(ml_dtypes.float8_e4m3fn).astype(np.float64)
    else:
        nib = np.empty((g, 128, n, 4), np.uint8)
        nib[..., 0::2] = words & 0xF
        nib[..., 1::2] = words >> 4
        vals = E2M1[nib]
    vals = vals * np.repeat(np.exp2(scales.astype(np.float64) - 127.0), 8, axis=1)[..., None]
    return vals.transpose(0, 1, 3, 2).reshape(g * 512, n)


def gelu(v):
    return 0.5 * v * (1.0 + np.tanh(np.sqrt(2.0 / np.pi) * (v + 0.044715 * v**3)))


K, M, T, S = 1536, 1024, 1024, 512


def setup_inputs():
    n = np.random.standard_normal
    s = mx_kscale(K)[:, None]
    w = n((K, M)) / np.sqrt(K) / s
    w4 = pack_weight(w, "e2m1")
    rest = w - unpack_weight(*w4, "e2m1")
    p_r8 = pack_weight(rest, "e4m3")
    return {
        "xT": (n((K, T)) * s).astype(np.float32),
        "w4_words": w4[0],
        "w4_scales": w4[1],
        "r8_words": p_r8[0],
        "r8_scales": p_r8[1],
        "wgt": np.repeat(np.random.uniform(0.5, 2.0, (8, S)), 16, axis=0).astype(np.float32),
        "b": (0.3 * n(1024)).astype(np.float32),
        "offs": striped8(np.stack([np.random.permutation(T)[:S] for _ in range(8)])),
    }


def reference(xT, w4_words, w4_scales, r8_words, r8_scales, wgt, b, offs):
    idx = unstriped8(offs)
    group = np.arange(K) % 512 // 64
    xg = f64(wgt)[np.arange(K) // 4 % 128] * f64(xT)[np.arange(K)[:, None], idx[group]]
    xT_ = mxq(xg, 0, "e4m3")
    w4_ = unpack_weight(w4_words, w4_scales, "e2m1")
    r8_ = unpack_weight(r8_words, r8_scales, "e4m3")
    y = xT_.T @ w4_ + xT_.T @ r8_
    return gelu(y + f64(b)[None, :])

@@ -1,0 +1,240 @@
+from contextlib import ExitStack
+
+import concourse.mybir as mybir
+from concourse.masks import make_identity
+
+K, M, T, S = 1536, 1024, 1024, 512
+FLOPS = 2 * 2 * K * M * S
+
+F32 = mybir.dt.float32
+BF16 = mybir.dt.bfloat16
+I32 = mybir.dt.int32
+U32 = mybir.dt.uint32
+U16 = mybir.dt.uint16
+U8 = mybir.dt.uint8
+FP8X4 = mybir.dt.float8_e4m3fn_x4
+FP4X4 = mybir.dt.float4_e2m1fn_x4
+ADD = mybir.AluOpType.add
+MULT = mybir.AluOpType.mult
+GELU = mybir.ActivationFunctionType.Gelu_apprx_tanh
+
+P = 128
+PACK = 4
+PASSES = K // (P * PACK)
+HALF = 512
+HALVES = M // HALF
+J_TILES = S // P
+MAIN = 384
+
+
+def tile_list_heads_tm_gelu_kernel(
+    tc, xT, w4_words, w4_scales, r8_words, r8_scales, wgt, b, offs, out
+):
+    nc = tc.nc
+    with ExitStack() as ctx:
+        held = ctx.enter_context(tc.tile_pool(name="held", bufs=1))
+        stage = ctx.enter_context(tc.tile_pool(name="stage", bufs=8))
+        psum = ctx.enter_context(tc.psum_pool(name="psum", bufs=1))
+
+        offsets = held.tile([P, S // 16], U16, name="offsets")
+        nc.sync.dma_start(offsets[:], offs)
+        factors = held.tile([P, S], F32, name="factors")
+        nc.sync.dma_start(factors[:, 0:256], wgt[:, 0:256])
+
+        w4_planes = held.tile([P, PASSES, M], U8, name="w4_planes", align_bytes=64)
+        r8_planes = held.tile([P, PASSES, M], U8, name="r8_planes", align_bytes=64)
+        nc.vector.memset(w4_planes[:].bitcast(I32), 0)
+        nc.vector.memset(r8_planes[:].bitcast(I32), 0)
+
+        b_cols = held.tile([P, M // P], F32, name="b_cols")
+        nc.scalar.dma_start(out=b_cols[:], in_=b.rearrange("(p c) -> p c", c=M // P))
+
+        warm = held.tile([P, 1], F32, name="warm")
+        nc.vector.memset(warm[:], 0.0)
+        nc.scalar.activation(warm[:], warm[:], GELU)
+
+        def load_scales(queue, all_planes, scales, q):
+            queue.dma_start(
+                out=all_planes[32 * q : 32 * q + 4, :, :].bitcast(I32),
+                in_=scales[:, 4 * q : 4 * q + 4, :].rearrange("a q n -> q a n").bitcast(I32),
+            )
+
+        ident = held.tile([P, P], F32, name="ident")
+        make_identity(nc, ident[:])
+
+        x = {}
+        r8 = []
+        w4 = []
+
+        def load_x(a, i):
+            plane = held.tile([P, T], F32, name="x%d_%d" % (a, i))
+            rows = xT[512 * a : 512 * (a + 1), :].rearrange("(p i) t -> p i t", i=PACK)
+            nc.sync.dma_start(out=plane[:], in_=rows[:, i, :])
+            x[a, i] = plane
+
+        def load_w(a, pieces):
+            r8_tile = held.tile([P, M], U32, name="r8_%d" % a, align_bytes=64)
+            w4_tile = held.tile([P, 2 * M], U8, name="w4_%d" % a, align_bytes=64)
+            r8.append(r8_tile)
+            w4.append(w4_tile)
+            for h in range(pieces):
+                n = M // pieces
+                if a == 0:
+                    load_scales(nc.sync, r8_planes, r8_scales, 0)
+                    load_scales(nc.sync, r8_planes, r8_scales, 1)
+                nc.sync.dma_start(
+                    out=w4_tile[:, 2 * n * h : 2 * n * (h + 1)].bitcast(I32),
+                    in_=w4_words[a][:, 2 * n * h : 2 * n * (h + 1)].bitcast(I32),
+                )
+                nc.sync.dma_start(
+                    out=r8_tile[:, n * h : n * (h + 1)].bitcast(I32),
+                    in_=r8_words[a].rearrange("p n t -> p (n t)")[:, 4 * n * h : 4 * n * (h + 1)].bitcast(I32),
+                )
+                if a == 0:
+                    load_scales(nc.sync, r8_planes, r8_scales, 2)
+                    load_scales(nc.sync, r8_planes, r8_scales, 3)
+
+        for a in range(PASSES):
+            for i in range(PACK):
+                load_x(a, i)
+                if a == 0 and i == 0:
+                    nc.sync.dma_start(factors[:, 256:S], wgt[:, 256:S])
+                if a == 0:
+                    load_scales(nc.sync, w4_planes, w4_scales, i)
+            load_w(a, 1)
+
+        banks = {}
+        for jt in range(J_TILES):
+            for h in range(HALVES):
+                banks[jt, h] = psum.tile([P, HALF], F32, name="bank%d_%d" % (jt, h))
+
+        bias = held.tile([P, M], F32, name="bias")
+        for g in range(2):
+            bank = banks[J_TILES - 1, g]
+            for c in range(4):
+                nc.tensor.transpose(
+                    bank[:, P * c : P * (c + 1)],
+                    b_cols[:, 4 * g + c : 4 * g + c + 1].to_broadcast([P, P]),
+                    ident[:],
+                )
+            nc.scalar.copy(
+                out=bias[:].rearrange("j (p c) -> j p c", c=8)[:, :, 4 * g : 4 * g + 4],
+                in_=bank[:].rearrange("j (c p) -> j p c", c=4),
+            )
+
+        picked = []
+        grouped = []
+        codes = []
+        planes = []
+        for a in range(PASSES):
+            picked.append(held.tile([P, PACK, S], F32, name="picked%d" % a))
+            grouped.append(held.tile([P, S, PACK], BF16, name="grouped%d" % a, align_bytes=64))
+            codes.append(held.tile([P, S], U32, name="codes%d" % a, align_bytes=64))
+            planes.append(held.tile([P, S], U8, name="planes%d" % a, align_bytes=64))
+
+        def gather(a, i, j0, j1):
+            nc.vector.tensor_tensor(
+                picked[a][:, i, j0:j1],
+                x[a, i][:].indirect(offsets[:, j0 // 16 : j1 // 16]),
+                factors[:, j0:j1],
+                MULT,
+            )
+
+        def interleave(a, j0, j1, i0=0, i1=PACK):
+            nc.scalar.copy(
+                out=grouped[a][:, j0:j1, i0:i1].rearrange("p (c u) i -> p c i u", u=4),
+                in_=picked[a][:, i0:i1, j0:j1].rearrange("p i (c u) -> p c i u", u=4),
+            )
+
+        def quantize(a, j0, j1):
+            nc.vector.quantize_mx(
+                out=codes[a][:, j0:j1].bitcast(FP8X4),
+                scales=planes[a][:, j0:j1],
+                in_=grouped[a][:, j0:j1, :].rearrange("p j i -> p (j i)"),
+            )
+
+        def multiply(a, jt, h):
+            j = slice(P * jt, P * (jt + 1))
+            n = slice(HALF * h, HALF * (h + 1))
+            nc.tensor.matmul_mx(
+                out=banks[jt, h][:],
+                lhsT=codes[a][:, j].bitcast(FP8X4),
+                lhsT_scale=planes[a][:, j],
+                rhs=w4[a][:, 2 * HALF * h : 2 * HALF * (h + 1)].bitcast(FP4X4),
+                rhs_scale=w4_planes[:, a, n],
+                start=(a == 0),
+                stop=False,
+            )
+            nc.tensor.matmul_mx(
+                out=banks[jt, h][:],
+                lhsT=codes[a][:, j].bitcast(FP8X4),
+                lhsT_scale=planes[a][:, j],
+                rhs=r8[a][:, n].bitcast(FP8X4),
+                rhs_scale=r8_planes[:, a, n],
+                start=False,
+                stop=(a == PASSES - 1),
+            )
+
+        def finish(jt, h):
+            n = slice(HALF * h, HALF * (h + 1))
+            y = stage.tile([P, HALF], F32, name="y")
+            o = stage.tile([P, HALF], F32, name="o")
+            pieces = 2 if (jt, h) == (J_TILES - 1, HALVES - 1) else 1
+            w = HALF // pieces
+            for c in range(0, HALF, w):
+                nc.vector.tensor_tensor(y[:, c : c + w], banks[jt, h][:, c : c + w], bias[:, HALF * h + c : HALF * h + c + w], ADD)
+                nc.scalar.activation(o[:, c : c + w], y[:, c : c + w], GELU)
+                nc.sync.dma_start(out=out[P * jt : P * (jt + 1), HALF * h + c : HALF * h + c + w], in_=o[:, c : c + w])
+
+        def multiply_tiles(a, tiles):
+            for h in range(HALVES):
+                for jt in tiles:
+                    multiply(a, jt, h)
+
+        A = (0, 256)
+        B = (256, S)
+        for a in (0, 1):
+            for i in range(PACK):
+                gather(a, i, *A)
+                if i % 2 == 1:
+                    interleave(a, *A, i - 1, i + 1)
+                gather(a, i, *B)
+                if i % 2 == 1:
+                    interleave(a, *B, i - 1, i + 1)
+                if a == 1 and i == 0:
+                    quantize(0, *B)
+                    multiply_tiles(0, (2, 3))
+            if a == 0:
+                quantize(0, *A)
+                multiply_tiles(0, (0, 1))
+        gather(2, 0, *A)
+        quantize(1, *A)
+        multiply_tiles(1, (0, 1))
+        gather(2, 1, *A)
+        interleave(2, *A, 0, 2)
+        quantize(1, *B)
+        multiply_tiles(1, (2, 3))
+        gather(2, 2, *A)
+        gather(2, 3, *A)
+        for jt in (0, 1):
+            interleave(2, P * jt, P * (jt + 1), 2, 4)
+        gather(2, 0, *B)
+        quantize(2, 0, P)
+        multiply_tiles(2, (0,))
+        gather(2, 1, *B)
+        interleave(2, *B, 0, 2)
+        quantize(2, P, 2 * P)
+        multiply_tiles(2, (1,))
+        gather(2, 2, *B)
+        gather(2, 3, *B)
+        for jt in (2, 3):
+            interleave(2, P * jt, P * (jt + 1), 2, 4)
+        finish(0, 0)
+        quantize(2, 2 * P, 3 * P)
+        multiply_tiles(2, (2,))
+        finish(0, 1)
+        quantize(2, 3 * P, S)
+        multiply_tiles(2, (3,))
+        for jt in range(1, J_TILES):
+            for h in range(HALVES):
+                finish(jt, h)

@@ -24,7 +24,7 @@ PASSES = K // (P * PACK)
 HALF = 512
 HALVES = M // HALF
 J_TILES = S // P
-MAIN = 384
+R8_ROW = 4
 
 
 def tile_list_heads_tm_gelu_kernel(
@@ -41,10 +41,8 @@ def tile_list_heads_tm_gelu_kernel(
         factors = held.tile([P, S], F32, name="factors")
         nc.sync.dma_start(factors[:, 0:256], wgt[:, 0:256])
 
-        w4_planes = held.tile([P, PASSES, M], U8, name="w4_planes", align_bytes=64)
-        r8_planes = held.tile([P, PASSES, M], U8, name="r8_planes", align_bytes=64)
-        nc.vector.memset(w4_planes[:].bitcast(I32), 0)
-        nc.vector.memset(r8_planes[:].bitcast(I32), 0)
+        w_planes = held.tile([P, PASSES, M], U8, name="w_planes", align_bytes=64)
+        nc.vector.memset(w_planes[:].bitcast(I32), 0)
 
         b_cols = held.tile([P, M // P], F32, name="b_cols")
         nc.scalar.dma_start(out=b_cols[:], in_=b.rearrange("(p c) -> p c", c=M // P))
@@ -53,18 +51,18 @@ def tile_list_heads_tm_gelu_kernel(
         nc.vector.memset(warm[:], 0.0)
         nc.scalar.activation(warm[:], warm[:], GELU)
 
-        def load_scales(queue, all_planes, scales, q):
-            queue.dma_start(
-                out=all_planes[32 * q : 32 * q + 4, :, :].bitcast(I32),
-                in_=scales[:, 4 * q : 4 * q + 4, :].rearrange("a q n -> q a n").bitcast(I32),
+        def load_scales(first_row, scales, r):
+            nc.sync.dma_start(
+                out=w_planes[first_row + r : P : 32, :, :].bitcast(I32),
+                in_=scales[:, r:16:4, :].rearrange("a q n -> q a n").bitcast(I32),
             )
 
         ident = held.tile([P, P], F32, name="ident")
         make_identity(nc, ident[:])
 
         x = {}
-        r8 = []
-        w4 = []
+        r8 = {}
+        w4 = {}
 
         def load_x(a, i):
             plane = held.tile([P, T], F32, name="x%d_%d" % (a, i))
@@ -72,36 +70,44 @@ def tile_list_heads_tm_gelu_kernel(
             nc.sync.dma_start(out=plane[:], in_=rows[:, i, :])
             x[a, i] = plane
 
-        def load_w(a, pieces):
-            r8_tile = held.tile([P, M], U32, name="r8_%d" % a, align_bytes=64)
-            w4_tile = held.tile([P, 2 * M], U8, name="w4_%d" % a, align_bytes=64)
-            r8.append(r8_tile)
-            w4.append(w4_tile)
+        def load_w4(a):
+            w4[a] = held.tile([P, 2 * M], U8, name="w4_%d" % a, align_bytes=64)
+            nc.sync.dma_start(out=w4[a][:].bitcast(I32), in_=w4_words[a].bitcast(I32))
+
+        def load_r8(a, pieces):
+            r8[a] = held.tile([P, M], U32, name="r8_%d" % a, align_bytes=64)
+            n = M // pieces
             for h in range(pieces):
-                n = M // pieces
-                if a == 0:
-                    load_scales(nc.sync, r8_planes, r8_scales, 0)
-                    load_scales(nc.sync, r8_planes, r8_scales, 1)
                 nc.sync.dma_start(
-                    out=w4_tile[:, 2 * n * h : 2 * n * (h + 1)].bitcast(I32),
-                    in_=w4_words[a][:, 2 * n * h : 2 * n * (h + 1)].bitcast(I32),
-                )
-                nc.sync.dma_start(
-                    out=r8_tile[:, n * h : n * (h + 1)].bitcast(I32),
+                    out=r8[a][:, n * h : n * (h + 1)].bitcast(I32),
                     in_=r8_words[a].rearrange("p n t -> p (n t)")[:, 4 * n * h : 4 * n * (h + 1)].bitcast(I32),
                 )
-                if a == 0:
-                    load_scales(nc.sync, r8_planes, r8_scales, 2)
-                    load_scales(nc.sync, r8_planes, r8_scales, 3)
 
-        for a in range(PASSES):
-            for i in range(PACK):
-                load_x(a, i)
-                if a == 0 and i == 0:
-                    nc.sync.dma_start(factors[:, 256:S], wgt[:, 256:S])
-                if a == 0:
-                    load_scales(nc.sync, w4_planes, w4_scales, i)
-            load_w(a, 1)
+        load_x(0, 0)
+        nc.sync.dma_start(factors[:, 256:S], wgt[:, 256:S])
+        for i in range(1, PACK):
+            load_x(0, i)
+        for r in range(4):
+            if r == 2:
+                load_x(1, 0)
+            load_scales(0, w4_scales, r)
+        load_x(1, 1)
+        load_w4(0)
+        load_scales(R8_ROW, r8_scales, 0)
+        load_scales(R8_ROW, r8_scales, 1)
+        load_x(1, 2)
+        load_scales(R8_ROW, r8_scales, 2)
+        load_scales(R8_ROW, r8_scales, 3)
+        load_r8(0, 1)
+        load_x(1, 3)
+        load_x(2, 0)
+        load_w4(1)
+        load_x(2, 1)
+        load_r8(1, 1)
+        load_x(2, 2)
+        load_x(2, 3)
+        load_w4(2)
+        load_r8(2, 2)
 
         banks = {}
         for jt in range(J_TILES):
@@ -153,30 +159,32 @@ def tile_list_heads_tm_gelu_kernel(
                 in_=grouped[a][:, j0:j1, :].rearrange("p j i -> p (j i)"),
             )
 
-        def multiply(a, jt, h):
+        def multiply_w4(a, jt, h):
+            j = slice(P * jt, P * (jt + 1))
+            nc.tensor.matmul_mx(
+                out=banks[jt, h][:],
+                lhsT=codes[a][:, j].bitcast(FP8X4),
+                lhsT_scale=planes[a][:, j],
+                rhs=w4[a][:, 2 * HALF * h : 2 * HALF * (h + 1)].bitcast(FP4X4),
+                rhs_scale=w_planes[:, a, HALF * h : HALF * (h + 1)],
+                start=(a == 0),
+                stop=False,
+            )
+
+        def multiply_r8(a, jt, h):
             j = slice(P * jt, P * (jt + 1))
             n = slice(HALF * h, HALF * (h + 1))
             nc.tensor.matmul_mx(
                 out=banks[jt, h][:],
                 lhsT=codes[a][:, j].bitcast(FP8X4),
                 lhsT_scale=planes[a][:, j],
-                rhs=w4[a][:, 2 * HALF * h : 2 * HALF * (h + 1)].bitcast(FP4X4),
-                rhs_scale=w4_planes[:, a, n],
-                start=(a == 0),
-                stop=False,
-            )
-            nc.tensor.matmul_mx(
-                out=banks[jt, h][:],
-                lhsT=codes[a][:, j].bitcast(FP8X4),
-                lhsT_scale=planes[a][:, j],
                 rhs=r8[a][:, n].bitcast(FP8X4),
-                rhs_scale=r8_planes[:, a, n],
+                rhs_scale=w_planes[R8_ROW:P, a, n],
                 start=False,
                 stop=(a == PASSES - 1),
             )
 
         def finish(jt, h):
-            n = slice(HALF * h, HALF * (h + 1))
             y = stage.tile([P, HALF], F32, name="y")
             o = stage.tile([P, HALF], F32, name="o")
             pieces = 2 if (jt, h) == (J_TILES - 1, HALVES - 1) else 1
@@ -186,55 +194,37 @@ def tile_list_heads_tm_gelu_kernel(
                 nc.scalar.activation(o[:, c : c + w], y[:, c : c + w], GELU)
                 nc.sync.dma_start(out=out[P * jt : P * (jt + 1), HALF * h + c : HALF * h + c + w], in_=o[:, c : c + w])
 
-        def multiply_tiles(a, tiles):
-            for h in range(HALVES):
+        def multiply_by_format(a, tiles):
+            for multiply in (multiply_w4, multiply_r8):
                 for jt in tiles:
-                    multiply(a, jt, h)
+                    for h in range(HALVES):
+                        multiply(a, jt, h)
 
-        A = (0, 256)
-        B = (256, S)
-        for a in (0, 1):
-            for i in range(PACK):
-                gather(a, i, *A)
-                if i % 2 == 1:
-                    interleave(a, *A, i - 1, i + 1)
-                gather(a, i, *B)
-                if i % 2 == 1:
-                    interleave(a, *B, i - 1, i + 1)
-                if a == 1 and i == 0:
-                    quantize(0, *B)
-                    multiply_tiles(0, (2, 3))
-            if a == 0:
-                quantize(0, *A)
-                multiply_tiles(0, (0, 1))
-        gather(2, 0, *A)
-        quantize(1, *A)
-        multiply_tiles(1, (0, 1))
-        gather(2, 1, *A)
-        interleave(2, *A, 0, 2)
-        quantize(1, *B)
-        multiply_tiles(1, (2, 3))
-        gather(2, 2, *A)
-        gather(2, 3, *A)
-        for jt in (0, 1):
-            interleave(2, P * jt, P * (jt + 1), 2, 4)
-        gather(2, 0, *B)
-        quantize(2, 0, P)
-        multiply_tiles(2, (0,))
-        gather(2, 1, *B)
-        interleave(2, *B, 0, 2)
-        quantize(2, P, 2 * P)
-        multiply_tiles(2, (1,))
-        gather(2, 2, *B)
-        gather(2, 3, *B)
-        for jt in (2, 3):
-            interleave(2, P * jt, P * (jt + 1), 2, 4)
-        finish(0, 0)
-        quantize(2, 2 * P, 3 * P)
-        multiply_tiles(2, (2,))
-        finish(0, 1)
-        quantize(2, 3 * P, S)
-        multiply_tiles(2, (3,))
-        for jt in range(1, J_TILES):
+        def second_pair(a, pieces):
+            w = S // pieces
+            gather(a, 2, 0, S)
+            for j0 in range(0, S, w):
+                gather(a, 3, j0, j0 + w)
+                interleave(a, j0, j0 + w, 2, 4)
+
+        gather(0, 0, 0, 256)
+        gather(0, 0, 256, S)
+        gather(0, 1, 0, S)
+        interleave(0, 0, S, 0, 2)
+        second_pair(0, 2)
+        for a in (1, 2):
+            gather(a, 0, 0, S)
+            quantize(a - 1, 0, 256)
+            quantize(a - 1, 256, S)
+            multiply_by_format(a - 1, range(J_TILES))
+            gather(a, 1, 0, S)
+            interleave(a, 0, S, 0, 2)
+            second_pair(a, 2 * a)
+        for jt in range(J_TILES):
+            quantize(2, P * jt, P * (jt + 1))
+            for h in range(HALVES):
+                multiply_w4(2, jt, h)
+                multiply_r8(2, jt, h)
+        for jt in range(J_TILES):
             for h in range(HALVES):
                 finish(jt, h)

@@ -25,6 +25,7 @@ HALF = 512
 HALVES = M // HALF
 J_TILES = S // P
 R8_ROW = 4
+LAST = PASSES - 1
 
 
 def tile_list_heads_tm_gelu_kernel(
@@ -39,10 +40,12 @@ def tile_list_heads_tm_gelu_kernel(
         offsets = held.tile([P, S // 16], U16, name="offsets")
         nc.sync.dma_start(offsets[:], offs)
         factors = held.tile([P, S], F32, name="factors")
-        nc.sync.dma_start(factors[:, 0:256], wgt[:, 0:256])
+        nc.sync.dma_start(factors[:], wgt)
 
-        w_planes = held.tile([P, PASSES, M], U8, name="w_planes", align_bytes=64)
-        nc.vector.memset(w_planes[:].bitcast(I32), 0)
+        w4_planes = held.tile([P, PASSES, M], U8, name="w4_planes", align_bytes=64)
+        r8_planes = held.tile([P, PASSES, M], U8, name="r8_planes", align_bytes=64)
+        nc.vector.memset(w4_planes[:].bitcast(I32), 0)
+        nc.vector.memset(r8_planes[:].bitcast(I32), 0)
 
         b_cols = held.tile([P, M // P], F32, name="b_cols")
         nc.scalar.dma_start(out=b_cols[:], in_=b.rearrange("(p c) -> p c", c=M // P))
@@ -51,7 +54,7 @@ def tile_list_heads_tm_gelu_kernel(
         nc.vector.memset(warm[:], 0.0)
         nc.scalar.activation(warm[:], warm[:], GELU)
 
-        def load_scales(first_row, scales, r):
+        def load_scales(w_planes, first_row, scales, r):
             nc.sync.dma_start(
                 out=w_planes[first_row + r : P : 32, :, :].bitcast(I32),
                 in_=scales[:, r:16:4, :].rearrange("a q n -> q a n").bitcast(I32),
@@ -84,21 +87,22 @@ def tile_list_heads_tm_gelu_kernel(
                 )
 
         load_x(0, 0)
-        nc.sync.dma_start(factors[:, 256:S], wgt[:, 256:S])
-        for i in range(1, PACK):
-            load_x(0, i)
-        for r in range(4):
-            if r == 2:
-                load_x(1, 0)
-            load_scales(0, w4_scales, r)
+        load_x(0, 1)
+        load_x(0, 2)
+        load_scales(w4_planes, 0, w4_scales, 0)
+        load_x(0, 3)
+        load_scales(w4_planes, 0, w4_scales, 1)
+        load_x(1, 0)
+        load_scales(w4_planes, 0, w4_scales, 2)
         load_x(1, 1)
+        load_scales(w4_planes, 0, w4_scales, 3)
         load_w4(0)
-        load_scales(R8_ROW, r8_scales, 0)
-        load_scales(R8_ROW, r8_scales, 1)
+        load_scales(r8_planes, R8_ROW, r8_scales, 0)
         load_x(1, 2)
-        load_scales(R8_ROW, r8_scales, 2)
-        load_scales(R8_ROW, r8_scales, 3)
+        load_scales(r8_planes, R8_ROW, r8_scales, 1)
         load_r8(0, 1)
+        load_scales(r8_planes, R8_ROW, r8_scales, 2)
+        load_scales(r8_planes, R8_ROW, r8_scales, 3)
         load_x(1, 3)
         load_x(2, 0)
         load_w4(1)
@@ -133,10 +137,15 @@ def tile_list_heads_tm_gelu_kernel(
         codes = []
         planes = []
         for a in range(PASSES):
-            picked.append(held.tile([P, PACK, S], F32, name="picked%d" % a))
+            picked.append(held.tile([P, PACK, S], F32, name="picked%d" % a, align_bytes=64))
             grouped.append(held.tile([P, S, PACK], BF16, name="grouped%d" % a, align_bytes=64))
             codes.append(held.tile([P, S], U32, name="codes%d" % a, align_bytes=64))
             planes.append(held.tile([P, S], U8, name="planes%d" % a, align_bytes=64))
+
+        borrowed = picked[LAST][:, PACK - 1, 2 * P : S].bitcast(BF16).rearrange("p (j i) -> p j i", i=PACK)
+
+        def group_of(a, j0, j1):
+            return borrowed if (a, j0) == (LAST, 0) else grouped[a][:, j0:j1, :]
 
         def gather(a, i, j0, j1):
             nc.vector.tensor_tensor(
@@ -148,7 +157,7 @@ def tile_list_heads_tm_gelu_kernel(
 
         def interleave(a, j0, j1, i0=0, i1=PACK):
             nc.scalar.copy(
-                out=grouped[a][:, j0:j1, i0:i1].rearrange("p (c u) i -> p c i u", u=4),
+                out=group_of(a, j0, j1)[:, :, i0:i1].rearrange("p (c u) i -> p c i u", u=4),
                 in_=picked[a][:, i0:i1, j0:j1].rearrange("p i (c u) -> p c i u", u=4),
             )
 
@@ -156,7 +165,7 @@ def tile_list_heads_tm_gelu_kernel(
             nc.vector.quantize_mx(
                 out=codes[a][:, j0:j1].bitcast(FP8X4),
                 scales=planes[a][:, j0:j1],
-                in_=grouped[a][:, j0:j1, :].rearrange("p j i -> p (j i)"),
+                in_=group_of(a, j0, j1).rearrange("p j i -> p (j i)"),
             )
 
         def multiply_w4(a, jt, h):
@@ -166,7 +175,7 @@ def tile_list_heads_tm_gelu_kernel(
                 lhsT=codes[a][:, j].bitcast(FP8X4),
                 lhsT_scale=planes[a][:, j],
                 rhs=w4[a][:, 2 * HALF * h : 2 * HALF * (h + 1)].bitcast(FP4X4),
-                rhs_scale=w_planes[:, a, HALF * h : HALF * (h + 1)],
+                rhs_scale=w4_planes[:, a, HALF * h : HALF * (h + 1)],
                 start=(a == 0),
                 stop=False,
             )
@@ -179,7 +188,7 @@ def tile_list_heads_tm_gelu_kernel(
                 lhsT=codes[a][:, j].bitcast(FP8X4),
                 lhsT_scale=planes[a][:, j],
                 rhs=r8[a][:, n].bitcast(FP8X4),
-                rhs_scale=w_planes[R8_ROW:P, a, n],
+                rhs_scale=r8_planes[R8_ROW:P, a, n],
                 start=False,
                 stop=(a == PASSES - 1),
             )
@@ -187,7 +196,7 @@ def tile_list_heads_tm_gelu_kernel(
         def finish(jt, h):
             y = stage.tile([P, HALF], F32, name="y")
             o = stage.tile([P, HALF], F32, name="o")
-            pieces = 2 if (jt, h) == (J_TILES - 1, HALVES - 1) else 1
+            pieces = 2 if (jt, h) in ((0, 0), (J_TILES - 1, HALVES - 1)) else 1
             w = HALF // pieces
             for c in range(0, HALF, w):
                 nc.vector.tensor_tensor(y[:, c : c + w], banks[jt, h][:, c : c + w], bias[:, HALF * h + c : HALF * h + c + w], ADD)
@@ -200,31 +209,38 @@ def tile_list_heads_tm_gelu_kernel(
                     for h in range(HALVES):
                         multiply(a, jt, h)
 
-        def second_pair(a, pieces):
-            w = S // pieces
-            gather(a, 2, 0, S)
-            for j0 in range(0, S, w):
-                gather(a, 3, j0, j0 + w)
-                interleave(a, j0, j0 + w, 2, 4)
-
-        gather(0, 0, 0, 256)
-        gather(0, 0, 256, S)
-        gather(0, 1, 0, S)
-        interleave(0, 0, S, 0, 2)
-        second_pair(0, 2)
-        for a in (1, 2):
-            gather(a, 0, 0, S)
-            quantize(a - 1, 0, 256)
-            quantize(a - 1, 256, S)
-            multiply_by_format(a - 1, range(J_TILES))
-            gather(a, 1, 0, S)
-            interleave(a, 0, S, 0, 2)
-            second_pair(a, 2 * a)
-        for jt in range(J_TILES):
-            quantize(2, P * jt, P * (jt + 1))
+        def multiply_tile(jt):
             for h in range(HALVES):
-                multiply_w4(2, jt, h)
-                multiply_r8(2, jt, h)
+                multiply_w4(LAST, jt, h)
+                multiply_r8(LAST, jt, h)
+
+        def last_plane(jt):
+            gather(LAST, 3, P * jt, P * (jt + 1))
+            interleave(LAST, P * jt, P * (jt + 1), 2, 4)
+
+        for a in range(PASSES):
+            gather(a, 0, 0, S)
+            if a > 0:
+                quantize(a - 1, 0, S // 2)
+                quantize(a - 1, S // 2, S)
+                multiply_by_format(a - 1, range(J_TILES))
+            gather(a, 1, 0, S)
+            if a < LAST:
+                interleave(a, 0, S, 0, 2)
+                gather(a, 2, 0, S)
+                for j0 in (0, S // 2):
+                    gather(a, 3, j0, j0 + S // 2)
+                    interleave(a, j0, j0 + S // 2, 2, 4)
+        interleave(LAST, 0, P, 0, 2)
+        interleave(LAST, P, S, 0, 2)
+        gather(LAST, 2, 0, S)
+        last_plane(0)
+        last_plane(1)
+        for jt in range(J_TILES):
+            quantize(LAST, P * jt, P * (jt + 1))
+            multiply_tile(jt)
+            if jt + 2 < J_TILES:
+                last_plane(jt + 2)
         for jt in range(J_TILES):
             for h in range(HALVES):
                 finish(jt, h)

@@ -43,9 +43,9 @@ def tile_list_heads_tm_gelu_kernel(
         nc.sync.dma_start(factors[:], wgt)
 
         w4_planes = held.tile([P, PASSES, M], U8, name="w4_planes", align_bytes=64)
-        r8_planes = held.tile([P, PASSES, M], U8, name="r8_planes", align_bytes=64)
-        nc.vector.memset(w4_planes[:].bitcast(I32), 0)
+        r8_planes = held.tile([P, M], U8, name="r8_planes", align_bytes=64)
         nc.vector.memset(r8_planes[:].bitcast(I32), 0)
+        nc.vector.memset(w4_planes[:].bitcast(I32), 0)
 
         b_cols = held.tile([P, M // P], F32, name="b_cols")
         nc.scalar.dma_start(out=b_cols[:], in_=b.rearrange("(p c) -> p c", c=M // P))
@@ -58,6 +58,12 @@ def tile_list_heads_tm_gelu_kernel(
             nc.sync.dma_start(
                 out=w_planes[first_row + r : P : 32, :, :].bitcast(I32),
                 in_=scales[:, r:16:4, :].rearrange("a q n -> q a n").bitcast(I32),
+            )
+
+        for q in range(4):
+            nc.gpsimd.dma_start(
+                out=r8_planes[32 * q + R8_ROW : 32 * q + R8_ROW * (PASSES + 1), :].bitcast(I32),
+                in_=r8_scales[:, 4 * q : 4 * q + 4, :].bitcast(I32),
             )
 
         ident = held.tile([P, P], F32, name="ident")
@@ -97,18 +103,14 @@ def tile_list_heads_tm_gelu_kernel(
         load_x(1, 1)
         load_scales(w4_planes, 0, w4_scales, 3)
         load_w4(0)
-        load_scales(r8_planes, R8_ROW, r8_scales, 0)
         load_x(1, 2)
-        load_scales(r8_planes, R8_ROW, r8_scales, 1)
         load_r8(0, 1)
-        load_scales(r8_planes, R8_ROW, r8_scales, 2)
-        load_scales(r8_planes, R8_ROW, r8_scales, 3)
         load_x(1, 3)
         load_x(2, 0)
         load_w4(1)
         load_x(2, 1)
-        load_r8(1, 1)
         load_x(2, 2)
+        load_r8(1, 1)
         load_x(2, 3)
         load_w4(2)
         load_r8(2, 2)
@@ -142,11 +144,6 @@ def tile_list_heads_tm_gelu_kernel(
             codes.append(held.tile([P, S], U32, name="codes%d" % a, align_bytes=64))
             planes.append(held.tile([P, S], U8, name="planes%d" % a, align_bytes=64))
 
-        borrowed = picked[LAST][:, PACK - 1, 2 * P : S].bitcast(BF16).rearrange("p (j i) -> p j i", i=PACK)
-
-        def group_of(a, j0, j1):
-            return borrowed if (a, j0) == (LAST, 0) else grouped[a][:, j0:j1, :]
-
         def gather(a, i, j0, j1):
             nc.vector.tensor_tensor(
                 picked[a][:, i, j0:j1],
@@ -157,7 +154,7 @@ def tile_list_heads_tm_gelu_kernel(
 
         def interleave(a, j0, j1, i0=0, i1=PACK):
             nc.scalar.copy(
-                out=group_of(a, j0, j1)[:, :, i0:i1].rearrange("p (c u) i -> p c i u", u=4),
+                out=grouped[a][:, j0:j1, i0:i1].rearrange("p (c u) i -> p c i u", u=4),
                 in_=picked[a][:, i0:i1, j0:j1].rearrange("p i (c u) -> p c i u", u=4),
             )
 
@@ -165,7 +162,7 @@ def tile_list_heads_tm_gelu_kernel(
             nc.vector.quantize_mx(
                 out=codes[a][:, j0:j1].bitcast(FP8X4),
                 scales=planes[a][:, j0:j1],
-                in_=group_of(a, j0, j1).rearrange("p j i -> p (j i)"),
+                in_=grouped[a][:, j0:j1, :].rearrange("p j i -> p (j i)"),
             )
 
         def multiply_w4(a, jt, h):
@@ -188,7 +185,7 @@ def tile_list_heads_tm_gelu_kernel(
                 lhsT=codes[a][:, j].bitcast(FP8X4),
                 lhsT_scale=planes[a][:, j],
                 rhs=r8[a][:, n].bitcast(FP8X4),
-                rhs_scale=r8_planes[R8_ROW:P, a, n],
+                rhs_scale=r8_planes[R8_ROW * (a + 1) : P, n],
                 start=False,
                 stop=(a == PASSES - 1),
             )
@@ -231,8 +228,7 @@ def tile_list_heads_tm_gelu_kernel(
                 for j0 in (0, S // 2):
                     gather(a, 3, j0, j0 + S // 2)
                     interleave(a, j0, j0 + S // 2, 2, 4)
-        interleave(LAST, 0, P, 0, 2)
-        interleave(LAST, P, S, 0, 2)
+        interleave(LAST, 0, S, 0, 2)
         gather(LAST, 2, 0, S)
         last_plane(0)
         last_plane(1)

@@ -79,18 +79,20 @@ def tile_list_heads_tm_gelu_kernel(
             nc.sync.dma_start(out=plane[:], in_=rows[:, i, :])
             x[a, i] = plane
 
-        def load_w4(a):
-            w4[a] = held.tile([P, 2 * M], U8, name="w4_%d" % a, align_bytes=64)
-            nc.sync.dma_start(out=w4[a][:].bitcast(I32), in_=w4_words[a].bitcast(I32))
+        def load_w4(a, n0, n1):
+            if n0 == 0:
+                w4[a] = held.tile([P, 2 * M], U8, name="w4_%d" % a, align_bytes=64)
+            nc.sync.dma_start(
+                out=w4[a][:, 2 * n0 : 2 * n1].bitcast(I32), in_=w4_words[a][:, 2 * n0 : 2 * n1].bitcast(I32)
+            )
 
-        def load_r8(a, pieces):
-            r8[a] = held.tile([P, M], U32, name="r8_%d" % a, align_bytes=64)
-            n = M // pieces
-            for h in range(pieces):
-                nc.sync.dma_start(
-                    out=r8[a][:, n * h : n * (h + 1)].bitcast(I32),
-                    in_=r8_words[a].rearrange("p n t -> p (n t)")[:, 4 * n * h : 4 * n * (h + 1)].bitcast(I32),
-                )
+        def load_r8(a, n0, n1):
+            if n0 == 0:
+                r8[a] = held.tile([P, M], U32, name="r8_%d" % a, align_bytes=64)
+            nc.sync.dma_start(
+                out=r8[a][:, n0:n1].bitcast(I32),
+                in_=r8_words[a].rearrange("p n t -> p (n t)")[:, 4 * n0 : 4 * n1].bitcast(I32),
+            )
 
         load_x(0, 0)
         load_x(0, 1)
@@ -102,18 +104,20 @@ def tile_list_heads_tm_gelu_kernel(
         load_scales(w4_planes, 0, w4_scales, 2)
         load_x(1, 1)
         load_scales(w4_planes, 0, w4_scales, 3)
-        load_w4(0)
+        load_w4(0, 0, M)
         load_x(1, 2)
-        load_r8(0, 1)
+        load_r8(0, 0, M)
         load_x(1, 3)
         load_x(2, 0)
-        load_w4(1)
+        load_w4(1, 0, M)
         load_x(2, 1)
         load_x(2, 2)
-        load_r8(1, 1)
+        load_r8(1, 0, HALF)
         load_x(2, 3)
-        load_w4(2)
-        load_r8(2, 2)
+        load_r8(1, HALF, M)
+        load_w4(2, 0, M)
+        load_r8(2, 0, HALF)
+        load_r8(2, HALF, M)
 
         banks = {}
         for jt in range(J_TILES):
@@ -144,9 +148,15 @@ def tile_list_heads_tm_gelu_kernel(
             codes.append(held.tile([P, S], U32, name="codes%d" % a, align_bytes=64))
             planes.append(held.tile([P, S], U8, name="planes%d" % a, align_bytes=64))
 
+        def pair_of(a, j0, j1, i0):
+            if (a, j1, i0) == (LAST, S, 2):
+                run = picked[a][:].rearrange("p i j -> p (i j)")[:, 2 * S + j0 : 2 * S + j0 + 2 * P]
+                return run.rearrange("p (i j) -> p i j", i=2)
+            return picked[a][:, i0 : i0 + 2, j0:j1]
+
         def gather(a, i, j0, j1):
             nc.vector.tensor_tensor(
-                picked[a][:, i, j0:j1],
+                pair_of(a, j0, j1, 2)[:, 1, :] if i == 3 else picked[a][:, i, j0:j1],
                 x[a, i][:].indirect(offsets[:, j0 // 16 : j1 // 16]),
                 factors[:, j0:j1],
                 MULT,
@@ -155,7 +165,7 @@ def tile_list_heads_tm_gelu_kernel(
         def interleave(a, j0, j1, i0=0, i1=PACK):
             nc.scalar.copy(
                 out=grouped[a][:, j0:j1, i0:i1].rearrange("p (c u) i -> p c i u", u=4),
-                in_=picked[a][:, i0:i1, j0:j1].rearrange("p i (c u) -> p c i u", u=4),
+                in_=pair_of(a, j0, j1, i0).rearrange("p i (c u) -> p c i u", u=4),
             )
 
         def quantize(a, j0, j1):
@@ -202,8 +212,8 @@ def tile_list_heads_tm_gelu_kernel(
 
         def multiply_by_format(a, tiles):
             for multiply in (multiply_w4, multiply_r8):
-                for jt in tiles:
-                    for h in range(HALVES):
+                for h in range(HALVES):
+                    for jt in tiles:
                         multiply(a, jt, h)
 
         def multiply_tile(jt):

@@ -38,9 +38,9 @@ def tile_list_heads_tm_gelu_kernel(
         psum = ctx.enter_context(tc.psum_pool(name="psum", bufs=1))
 
         offsets = held.tile([P, S // 16], U16, name="offsets")
-        nc.sync.dma_start(offsets[:], offs)
         factors = held.tile([P, S], F32, name="factors")
         nc.sync.dma_start(factors[:], wgt)
+        nc.sync.dma_start(offsets[:], offs)
 
         w4_planes = held.tile([P, PASSES, M], U8, name="w4_planes", align_bytes=64)
         r8_planes = held.tile([P, M], U8, name="r8_planes", align_bytes=64)
@@ -96,10 +96,10 @@ def tile_list_heads_tm_gelu_kernel(
 
         load_x(0, 0)
         load_x(0, 1)
-        load_x(0, 2)
         load_scales(w4_planes, 0, w4_scales, 0)
-        load_x(0, 3)
+        load_x(0, 2)
         load_scales(w4_planes, 0, w4_scales, 1)
+        load_x(0, 3)
         load_x(1, 0)
         load_scales(w4_planes, 0, w4_scales, 2)
         load_x(1, 1)
@@ -148,15 +148,9 @@ def tile_list_heads_tm_gelu_kernel(
             codes.append(held.tile([P, S], U32, name="codes%d" % a, align_bytes=64))
             planes.append(held.tile([P, S], U8, name="planes%d" % a, align_bytes=64))
 
-        def pair_of(a, j0, j1, i0):
-            if (a, j1, i0) == (LAST, S, 2):
-                run = picked[a][:].rearrange("p i j -> p (i j)")[:, 2 * S + j0 : 2 * S + j0 + 2 * P]
-                return run.rearrange("p (i j) -> p i j", i=2)
-            return picked[a][:, i0 : i0 + 2, j0:j1]
-
         def gather(a, i, j0, j1):
             nc.vector.tensor_tensor(
-                pair_of(a, j0, j1, 2)[:, 1, :] if i == 3 else picked[a][:, i, j0:j1],
+                picked[a][:, i, j0:j1],
                 x[a, i][:].indirect(offsets[:, j0 // 16 : j1 // 16]),
                 factors[:, j0:j1],
                 MULT,
@@ -165,7 +159,7 @@ def tile_list_heads_tm_gelu_kernel(
         def interleave(a, j0, j1, i0=0, i1=PACK):
             nc.scalar.copy(
                 out=grouped[a][:, j0:j1, i0:i1].rearrange("p (c u) i -> p c i u", u=4),
-                in_=pair_of(a, j0, j1, i0).rearrange("p i (c u) -> p c i u", u=4),
+                in_=picked[a][:, i0:i1, j0:j1].rearrange("p i (c u) -> p c i u", u=4),
             )
 
         def quantize(a, j0, j1):
@@ -203,12 +197,15 @@ def tile_list_heads_tm_gelu_kernel(
         def finish(jt, h):
             y = stage.tile([P, HALF], F32, name="y")
             o = stage.tile([P, HALF], F32, name="o")
-            pieces = 2 if (jt, h) in ((0, 0), (J_TILES - 1, HALVES - 1)) else 1
-            w = HALF // pieces
-            for c in range(0, HALF, w):
-                nc.vector.tensor_tensor(y[:, c : c + w], banks[jt, h][:, c : c + w], bias[:, HALF * h + c : HALF * h + c + w], ADD)
-                nc.scalar.activation(o[:, c : c + w], y[:, c : c + w], GELU)
-                nc.sync.dma_start(out=out[P * jt : P * (jt + 1), HALF * h + c : HALF * h + c + w], in_=o[:, c : c + w])
+            first, last = (jt, h) == (0, 0), (jt, h) == (J_TILES - 1, HALVES - 1)
+            rows = out[P * jt : P * (jt + 1), HALF * h : HALF * (h + 1)]
+            for c in (slice(0, HALF // 2), slice(HALF // 2, HALF)):
+                nc.vector.tensor_tensor(y[:, c], banks[jt, h][:, c], bias[:, HALF * h : HALF * (h + 1)][:, c], ADD)
+                nc.scalar.activation(o[:, c], y[:, c], GELU)
+                if first or last:
+                    nc.sync.dma_start(out=rows[:, c], in_=o[:, c])
+            if not (first or last):
+                nc.sync.dma_start(out=rows, in_=o[:])
 
         def multiply_by_format(a, tiles):
             for multiply in (multiply_w4, multiply_r8):

@@ -47,7 +47,7 @@ def tile_list_heads_tm_gelu_kernel(
         nc.vector.memset(r8_planes[:].bitcast(I32), 0)
         nc.vector.memset(w4_planes[:].bitcast(I32), 0)
 
-        b_cols = held.tile([P, M // P], F32, name="b_cols")
+        b_cols = held.tile([P, M // P], F32, name="b_cols", tag="grouped0", align_bytes=64)
         nc.scalar.dma_start(out=b_cols[:], in_=b.rearrange("(p c) -> p c", c=M // P))
 
         warm = held.tile([P, 1], F32, name="warm")
@@ -144,7 +144,7 @@ def tile_list_heads_tm_gelu_kernel(
         planes = []
         for a in range(PASSES):
             picked.append(held.tile([P, PACK, S], F32, name="picked%d" % a, align_bytes=64))
-            grouped.append(held.tile([P, S, PACK], BF16, name="grouped%d" % a, align_bytes=64))
+            grouped.append(held.tile([P, S, PACK], BF16, name="grouped%d" % a, tag="grouped%d" % a, align_bytes=64))
             codes.append(held.tile([P, S], U32, name="codes%d" % a, align_bytes=64))
             planes.append(held.tile([P, S], U8, name="planes%d" % a, align_bytes=64))
 

@@ -102,9 +102,9 @@ def tile_list_heads_tm_gelu_kernel(
         load_x(0, 3)
         load_x(1, 0)
         load_scales(w4_planes, 0, w4_scales, 2)
-        load_x(1, 1)
         load_scales(w4_planes, 0, w4_scales, 3)
         load_w4(0, 0, M)
+        load_x(1, 1)
         load_x(1, 2)
         load_r8(0, 0, M)
         load_x(1, 3)

@@ -21,11 +21,10 @@ GELU = mybir.ActivationFunctionType.Gelu_apprx_tanh
 P = 128
 PACK = 4
 PASSES = K // (P * PACK)
-HALF = 512
-HALVES = M // HALF
-J_TILES = S // P
-R8_ROW = 4
 LAST = PASSES - 1
+BANK = 512
+TILES = S // P
+QUAD_ROWS = 4
 
 
 def tile_list_heads_tm_gelu_kernel(
@@ -37,129 +36,115 @@ def tile_list_heads_tm_gelu_kernel(
         stage = ctx.enter_context(tc.tile_pool(name="stage", bufs=8))
         psum = ctx.enter_context(tc.psum_pool(name="psum", bufs=1))
 
-        offsets = held.tile([P, S // 16], U16, name="offsets")
         factors = held.tile([P, S], F32, name="factors")
+        offsets = held.tile([P, S // 16], U16, name="offsets")
+        b_cols = held.tile([P, M // P], F32, name="b_cols", tag="grouped0", align_bytes=64)
         nc.sync.dma_start(factors[:], wgt)
         nc.sync.dma_start(offsets[:], offs)
+        nc.scalar.dma_start(out=b_cols[:], in_=b.rearrange("(p c) -> p c", c=M // P))
 
         w4_planes = held.tile([P, PASSES, M], U8, name="w4_planes", align_bytes=64)
         r8_planes = held.tile([P, M], U8, name="r8_planes", align_bytes=64)
         nc.vector.memset(r8_planes[:].bitcast(I32), 0)
         nc.vector.memset(w4_planes[:].bitcast(I32), 0)
 
-        b_cols = held.tile([P, M // P], F32, name="b_cols", tag="grouped0", align_bytes=64)
-        nc.scalar.dma_start(out=b_cols[:], in_=b.rearrange("(p c) -> p c", c=M // P))
-
         warm = held.tile([P, 1], F32, name="warm")
         nc.vector.memset(warm[:], 0.0)
         nc.scalar.activation(warm[:], warm[:], GELU)
 
-        def load_scales(w_planes, first_row, scales, r):
-            nc.sync.dma_start(
-                out=w_planes[first_row + r : P : 32, :, :].bitcast(I32),
-                in_=scales[:, r:16:4, :].rearrange("a q n -> q a n").bitcast(I32),
-            )
-
         for q in range(4):
             nc.gpsimd.dma_start(
-                out=r8_planes[32 * q + R8_ROW : 32 * q + R8_ROW * (PASSES + 1), :].bitcast(I32),
+                out=r8_planes[32 * q + QUAD_ROWS : 32 * q + QUAD_ROWS * (PASSES + 1), :].bitcast(I32),
                 in_=r8_scales[:, 4 * q : 4 * q + 4, :].bitcast(I32),
             )
-
         ident = held.tile([P, P], F32, name="ident")
         make_identity(nc, ident[:])
 
         x = {}
-        r8 = {}
-        w4 = {}
+        w4 = [held.tile([P, 2 * M], U8, name="w4_%d" % a, align_bytes=64) for a in range(PASSES)]
+        r8 = [held.tile([P, M], U32, name="r8_%d" % a, align_bytes=64) for a in range(PASSES)]
 
-        def load_x(a, i):
-            plane = held.tile([P, T], F32, name="x%d_%d" % (a, i))
+        def load_plane(a, i):
+            x[a, i] = held.tile([P, T], F32, name="x%d_%d" % (a, i))
             rows = xT[512 * a : 512 * (a + 1), :].rearrange("(p i) t -> p i t", i=PACK)
-            nc.sync.dma_start(out=plane[:], in_=rows[:, i, :])
-            x[a, i] = plane
+            nc.sync.dma_start(out=x[a, i][:], in_=rows[:, i, :])
+
+        def load_w4_scales(r):
+            nc.sync.dma_start(
+                out=w4_planes[r:P:32, :, :].bitcast(I32),
+                in_=w4_scales[:, r:16:4, :].rearrange("a q n -> q a n").bitcast(I32),
+            )
 
         def load_w4(a, n0, n1):
-            if n0 == 0:
-                w4[a] = held.tile([P, 2 * M], U8, name="w4_%d" % a, align_bytes=64)
             nc.sync.dma_start(
                 out=w4[a][:, 2 * n0 : 2 * n1].bitcast(I32), in_=w4_words[a][:, 2 * n0 : 2 * n1].bitcast(I32)
             )
 
         def load_r8(a, n0, n1):
-            if n0 == 0:
-                r8[a] = held.tile([P, M], U32, name="r8_%d" % a, align_bytes=64)
             nc.sync.dma_start(
                 out=r8[a][:, n0:n1].bitcast(I32),
                 in_=r8_words[a].rearrange("p n t -> p (n t)")[:, 4 * n0 : 4 * n1].bitcast(I32),
             )
 
-        load_x(0, 0)
-        load_x(0, 1)
-        load_scales(w4_planes, 0, w4_scales, 0)
-        load_x(0, 2)
-        load_scales(w4_planes, 0, w4_scales, 1)
-        load_x(0, 3)
-        load_x(1, 0)
-        load_scales(w4_planes, 0, w4_scales, 2)
-        load_scales(w4_planes, 0, w4_scales, 3)
+        load_plane(0, 0)
+        load_plane(0, 1)
+        load_w4_scales(0)
+        load_plane(0, 2)
+        load_w4_scales(1)
+        load_plane(0, 3)
+        load_plane(1, 0)
+        load_w4_scales(2)
+        load_plane(1, 1)
+        load_w4_scales(3)
         load_w4(0, 0, M)
-        load_x(1, 1)
-        load_x(1, 2)
-        load_r8(0, 0, M)
-        load_x(1, 3)
-        load_x(2, 0)
+        load_plane(1, 2)
+        load_r8(0, 0, BANK)
+        load_plane(1, 3)
+        load_plane(2, 0)
+        load_r8(0, BANK, M)
         load_w4(1, 0, M)
-        load_x(2, 1)
-        load_x(2, 2)
-        load_r8(1, 0, HALF)
-        load_x(2, 3)
-        load_r8(1, HALF, M)
+        load_plane(2, 1)
+        load_plane(2, 2)
+        load_plane(2, 3)
+        load_r8(1, 0, BANK)
         load_w4(2, 0, M)
-        load_r8(2, 0, HALF)
-        load_r8(2, HALF, M)
+        load_r8(2, 0, BANK)
+        load_r8(1, BANK, M)
+        load_r8(2, BANK, M)
 
         banks = {}
-        for jt in range(J_TILES):
-            for h in range(HALVES):
-                banks[jt, h] = psum.tile([P, HALF], F32, name="bank%d_%d" % (jt, h))
+        for h in range(2):
+            for jt in range(TILES):
+                banks[jt, h] = psum.tile([P, BANK], F32, name="bank%d_%d" % (jt, h))
 
         bias = held.tile([P, M], F32, name="bias")
         for g in range(2):
-            bank = banks[J_TILES - 1, g]
+            bank = banks[TILES - 1, g]
             for c in range(4):
-                nc.tensor.transpose(
-                    bank[:, P * c : P * (c + 1)],
-                    b_cols[:, 4 * g + c : 4 * g + c + 1].to_broadcast([P, P]),
-                    ident[:],
-                )
+                column = b_cols[:, 4 * g + c : 4 * g + c + 1]
+                nc.tensor.transpose(bank[:, P * c : P * (c + 1)], column.to_broadcast([P, P]), ident[:])
             nc.scalar.copy(
                 out=bias[:].rearrange("j (p c) -> j p c", c=8)[:, :, 4 * g : 4 * g + 4],
                 in_=bank[:].rearrange("j (c p) -> j p c", c=4),
             )
 
-        picked = []
-        grouped = []
-        codes = []
-        planes = []
-        for a in range(PASSES):
-            picked.append(held.tile([P, PACK, S], F32, name="picked%d" % a, align_bytes=64))
-            grouped.append(held.tile([P, S, PACK], BF16, name="grouped%d" % a, tag="grouped%d" % a, align_bytes=64))
-            codes.append(held.tile([P, S], U32, name="codes%d" % a, align_bytes=64))
-            planes.append(held.tile([P, S], U8, name="planes%d" % a, align_bytes=64))
+        picked = [held.tile([P, PACK, S], F32, name="picked%d" % a, align_bytes=64) for a in range(PASSES)]
+        grouped = [
+            held.tile([P, S, PACK], BF16, name="grouped%d" % a, tag="grouped%d" % a, align_bytes=64)
+            for a in range(PASSES)
+        ]
+        codes = [held.tile([P, S], U32, name="codes%d" % a, align_bytes=64) for a in range(PASSES)]
+        planes = [held.tile([P, S], U8, name="planes%d" % a, align_bytes=64) for a in range(PASSES)]
 
-        def gather(a, i, j0, j1):
-            nc.vector.tensor_tensor(
-                picked[a][:, i, j0:j1],
-                x[a, i][:].indirect(offsets[:, j0 // 16 : j1 // 16]),
-                factors[:, j0:j1],
-                MULT,
-            )
+        def gather(a, i, j0=0, j1=S):
+            window = x[a, i][:].indirect(offsets[:, j0 // 16 : j1 // 16])
+            nc.vector.tensor_tensor(picked[a][:, i, j0:j1], window, factors[:, j0:j1], MULT)
 
-        def interleave(a, j0, j1, i0=0, i1=PACK):
+        def interleave(a, pair, j0=0, j1=S):
+            i = slice(2 * pair, 2 * pair + 2)
             nc.scalar.copy(
-                out=grouped[a][:, j0:j1, i0:i1].rearrange("p (c u) i -> p c i u", u=4),
-                in_=picked[a][:, i0:i1, j0:j1].rearrange("p i (c u) -> p c i u", u=4),
+                out=grouped[a][:, j0:j1, i].rearrange("p (c u) i -> p c i u", u=4),
+                in_=picked[a][:, i, j0:j1].rearrange("p i (c u) -> p c i u", u=4),
             )
 
         def quantize(a, j0, j1):
@@ -175,75 +160,78 @@ def tile_list_heads_tm_gelu_kernel(
                 out=banks[jt, h][:],
                 lhsT=codes[a][:, j].bitcast(FP8X4),
                 lhsT_scale=planes[a][:, j],
-                rhs=w4[a][:, 2 * HALF * h : 2 * HALF * (h + 1)].bitcast(FP4X4),
-                rhs_scale=w4_planes[:, a, HALF * h : HALF * (h + 1)],
+                rhs=w4[a][:, 2 * BANK * h : 2 * BANK * (h + 1)].bitcast(FP4X4),
+                rhs_scale=w4_planes[:, a, BANK * h : BANK * (h + 1)],
                 start=(a == 0),
                 stop=False,
             )
 
         def multiply_r8(a, jt, h):
             j = slice(P * jt, P * (jt + 1))
-            n = slice(HALF * h, HALF * (h + 1))
+            n = slice(BANK * h, BANK * (h + 1))
             nc.tensor.matmul_mx(
                 out=banks[jt, h][:],
                 lhsT=codes[a][:, j].bitcast(FP8X4),
                 lhsT_scale=planes[a][:, j],
                 rhs=r8[a][:, n].bitcast(FP8X4),
-                rhs_scale=r8_planes[R8_ROW * (a + 1) : P, n],
+                rhs_scale=r8_planes[QUAD_ROWS * (a + 1) : P, n],
                 start=False,
-                stop=(a == PASSES - 1),
+                stop=(a == LAST),
             )
 
+        def sweep(multiply, a, halves):
+            for h in halves:
+                for jt in range(TILES):
+                    multiply(a, jt, h)
+
         def finish(jt, h):
-            y = stage.tile([P, HALF], F32, name="y")
-            o = stage.tile([P, HALF], F32, name="o")
-            first, last = (jt, h) == (0, 0), (jt, h) == (J_TILES - 1, HALVES - 1)
-            rows = out[P * jt : P * (jt + 1), HALF * h : HALF * (h + 1)]
-            for c in (slice(0, HALF // 2), slice(HALF // 2, HALF)):
-                nc.vector.tensor_tensor(y[:, c], banks[jt, h][:, c], bias[:, HALF * h : HALF * (h + 1)][:, c], ADD)
+            y = stage.tile([P, BANK], F32, name="y")
+            o = stage.tile([P, BANK], F32, name="o")
+            in_halves = (jt, h) in ((0, 0), (TILES - 1, 1))
+            rows = out[P * jt : P * (jt + 1), BANK * h : BANK * (h + 1)]
+            cuts = (0, 256, 384, 512) if (jt, h) == (TILES - 1, 1) else (0, 256, 512)
+            for c in (slice(c0, c1) for c0, c1 in zip(cuts, cuts[1:])):
+                nc.vector.tensor_tensor(y[:, c], banks[jt, h][:, c], bias[:, BANK * h : BANK * (h + 1)][:, c], ADD)
                 nc.scalar.activation(o[:, c], y[:, c], GELU)
-                if first or last:
+                if in_halves:
                     nc.sync.dma_start(out=rows[:, c], in_=o[:, c])
-            if not (first or last):
+            if not in_halves:
                 nc.sync.dma_start(out=rows, in_=o[:])
-
-        def multiply_by_format(a, tiles):
-            for multiply in (multiply_w4, multiply_r8):
-                for h in range(HALVES):
-                    for jt in tiles:
-                        multiply(a, jt, h)
-
-        def multiply_tile(jt):
-            for h in range(HALVES):
-                multiply_w4(LAST, jt, h)
-                multiply_r8(LAST, jt, h)
 
         def last_plane(jt):
             gather(LAST, 3, P * jt, P * (jt + 1))
-            interleave(LAST, P * jt, P * (jt + 1), 2, 4)
+            interleave(LAST, 1, P * jt, P * (jt + 1))
 
         for a in range(PASSES):
-            gather(a, 0, 0, S)
+            gather(a, 0)
             if a > 0:
                 quantize(a - 1, 0, S // 2)
                 quantize(a - 1, S // 2, S)
-                multiply_by_format(a - 1, range(J_TILES))
-            gather(a, 1, 0, S)
+            if a == 1:
+                sweep(multiply_w4, 0, (0, 1))
+                sweep(multiply_r8, 0, (0, 1))
+            if a == 2:
+                sweep(multiply_w4, 1, (0, 1))
+                sweep(multiply_r8, 1, (0,))
+            gather(a, 1)
+            interleave(a, 0)
+            gather(a, 2)
             if a < LAST:
-                interleave(a, 0, S, 0, 2)
-                gather(a, 2, 0, S)
                 for j0 in (0, S // 2):
                     gather(a, 3, j0, j0 + S // 2)
-                    interleave(a, j0, j0 + S // 2, 2, 4)
-        interleave(LAST, 0, S, 0, 2)
-        gather(LAST, 2, 0, S)
+                    interleave(a, 1, j0, j0 + S // 2)
         last_plane(0)
         last_plane(1)
-        for jt in range(J_TILES):
+        for jt in range(TILES):
             quantize(LAST, P * jt, P * (jt + 1))
-            multiply_tile(jt)
-            if jt + 2 < J_TILES:
+            multiply_w4(LAST, jt, 0)
+            multiply_r8(LAST, jt, 0)
+            if jt + 2 < TILES:
                 last_plane(jt + 2)
-        for jt in range(J_TILES):
-            for h in range(HALVES):
+        for jt in range(TILES):
+            multiply_w4(LAST, jt, 1)
+            multiply_r8(1, jt, 1)
+            multiply_r8(LAST, jt, 1)
+        for h in range(2):
+            for jt in range(TILES):
                 finish(jt, h)

@@ -23,6 +23,7 @@ PACK = 4
 PASSES = K // (P * PACK)
 LAST = PASSES - 1
 BANK = 512
+QUARTER = M // 4
 TILES = S // P
 QUAD_ROWS = 4
 
@@ -105,11 +106,13 @@ def tile_list_heads_tm_gelu_kernel(
         load_w4(1, 0, M)
         load_plane(2, 1)
         load_plane(2, 2)
+        load_r8(1, 0, QUARTER)
         load_plane(2, 3)
-        load_r8(1, 0, BANK)
+        load_r8(1, QUARTER, 2 * QUARTER)
+        load_r8(1, 2 * QUARTER, 3 * QUARTER)
         load_w4(2, 0, M)
         load_r8(2, 0, BANK)
-        load_r8(1, BANK, M)
+        load_r8(1, 3 * QUARTER, M)
         load_r8(2, BANK, M)
 
         banks = {}
@@ -166,11 +169,11 @@ def tile_list_heads_tm_gelu_kernel(
                 stop=False,
             )
 
-        def multiply_r8(a, jt, h):
+        def multiply_r8(a, jt, h, c0=0, c1=BANK):
             j = slice(P * jt, P * (jt + 1))
-            n = slice(BANK * h, BANK * (h + 1))
+            n = slice(BANK * h + c0, BANK * h + c1)
             nc.tensor.matmul_mx(
-                out=banks[jt, h][:],
+                out=banks[jt, h][:, c0:c1],
                 lhsT=codes[a][:, j].bitcast(FP8X4),
                 lhsT_scale=planes[a][:, j],
                 rhs=r8[a][:, n].bitcast(FP8X4),
@@ -189,8 +192,7 @@ def tile_list_heads_tm_gelu_kernel(
             o = stage.tile([P, BANK], F32, name="o")
             in_halves = (jt, h) in ((0, 0), (TILES - 1, 1))
             rows = out[P * jt : P * (jt + 1), BANK * h : BANK * (h + 1)]
-            cuts = (0, 256, 384, 512) if (jt, h) == (TILES - 1, 1) else (0, 256, 512)
-            for c in (slice(c0, c1) for c0, c1 in zip(cuts, cuts[1:])):
+            for c in (slice(0, BANK // 2), slice(BANK // 2, BANK)):
                 nc.vector.tensor_tensor(y[:, c], banks[jt, h][:, c], bias[:, BANK * h : BANK * (h + 1)][:, c], ADD)
                 nc.scalar.activation(o[:, c], y[:, c], GELU)
                 if in_halves:
@@ -212,7 +214,9 @@ def tile_list_heads_tm_gelu_kernel(
                 sweep(multiply_r8, 0, (0, 1))
             if a == 2:
                 sweep(multiply_w4, 1, (0, 1))
-                sweep(multiply_r8, 1, (0,))
+                for h, c0 in ((0, 0), (0, QUARTER), (1, 0)):
+                    for jt in range(TILES):
+                        multiply_r8(1, jt, h, c0, c0 + QUARTER)
             gather(a, 1)
             interleave(a, 0)
             gather(a, 2)
@@ -230,7 +234,7 @@ def tile_list_heads_tm_gelu_kernel(
                 last_plane(jt + 2)
         for jt in range(TILES):
             multiply_w4(LAST, jt, 1)
-            multiply_r8(1, jt, 1)
+            multiply_r8(1, jt, 1, QUARTER, BANK)
             multiply_r8(LAST, jt, 1)
         for h in range(2):
             for jt in range(TILES):

@@ -109,10 +109,10 @@ def tile_list_heads_tm_gelu_kernel(
         load_r8(1, 0, QUARTER)
         load_plane(2, 3)
         load_r8(1, QUARTER, 2 * QUARTER)
-        load_r8(1, 2 * QUARTER, 3 * QUARTER)
-        load_w4(2, 0, M)
+        load_r8(1, BANK, M)
+        load_w4(2, 0, BANK)
         load_r8(2, 0, BANK)
-        load_r8(1, 3 * QUARTER, M)
+        load_w4(2, BANK, M)
         load_r8(2, BANK, M)
 
         banks = {}
@@ -214,9 +214,10 @@ def tile_list_heads_tm_gelu_kernel(
                 sweep(multiply_r8, 0, (0, 1))
             if a == 2:
                 sweep(multiply_w4, 1, (0, 1))
-                for h, c0 in ((0, 0), (0, QUARTER), (1, 0)):
+                for c0 in (0, QUARTER):
                     for jt in range(TILES):
-                        multiply_r8(1, jt, h, c0, c0 + QUARTER)
+                        multiply_r8(1, jt, 0, c0, c0 + QUARTER)
+                sweep(multiply_r8, 1, (1,))
             gather(a, 1)
             interleave(a, 0)
             gather(a, 2)
@@ -234,7 +235,6 @@ def tile_list_heads_tm_gelu_kernel(
                 last_plane(jt + 2)
         for jt in range(TILES):
             multiply_w4(LAST, jt, 1)
-            multiply_r8(1, jt, 1, QUARTER, BANK)
             multiply_r8(LAST, jt, 1)
         for h in range(2):
             for jt in range(TILES):

@@ -106,9 +106,8 @@ def tile_list_heads_tm_gelu_kernel(
         load_w4(1, 0, M)
         load_plane(2, 1)
         load_plane(2, 2)
-        load_r8(1, 0, QUARTER)
+        load_r8(1, 0, BANK)
         load_plane(2, 3)
-        load_r8(1, QUARTER, 2 * QUARTER)
         load_r8(1, BANK, M)
         load_w4(2, 0, BANK)
         load_r8(2, 0, BANK)
@@ -214,10 +213,7 @@ def tile_list_heads_tm_gelu_kernel(
                 sweep(multiply_r8, 0, (0, 1))
             if a == 2:
                 sweep(multiply_w4, 1, (0, 1))
-                for c0 in (0, QUARTER):
-                    for jt in range(TILES):
-                        multiply_r8(1, jt, 0, c0, c0 + QUARTER)
-                sweep(multiply_r8, 1, (1,))
+                sweep(multiply_r8, 1, (0, 1))
             gather(a, 1)
             interleave(a, 0)
             gather(a, 2)

@@ -44,8 +44,8 @@ def tile_list_heads_tm_gelu_kernel(
         nc.sync.dma_start(offsets[:], offs)
         nc.scalar.dma_start(out=b_cols[:], in_=b.rearrange("(p c) -> p c", c=M // P))
 
-        w4_planes = held.tile([P, PASSES, M], U8, name="w4_planes", align_bytes=64)
-        r8_planes = held.tile([P, M], U8, name="r8_planes", align_bytes=64)
+        w4_planes = held.tile([P, PASSES, M], U8, name="w4_planes", align_bytes=256)
+        r8_planes = held.tile([P, M], U8, name="r8_planes", align_bytes=256)
         nc.vector.memset(r8_planes[:].bitcast(I32), 0)
         nc.vector.memset(w4_planes[:].bitcast(I32), 0)
 
@@ -62,11 +62,11 @@ def tile_list_heads_tm_gelu_kernel(
         make_identity(nc, ident[:])
 
         x = {}
-        w4 = [held.tile([P, 2 * M], U8, name="w4_%d" % a, align_bytes=64) for a in range(PASSES)]
-        r8 = [held.tile([P, M], U32, name="r8_%d" % a, align_bytes=64) for a in range(PASSES)]
+        w4 = [held.tile([P, 2 * M], U8, name="w4_%d" % a, align_bytes=256) for a in range(PASSES)]
+        r8 = [held.tile([P, M], U32, name="r8_%d" % a, align_bytes=256) for a in range(PASSES)]
 
         def load_plane(a, i):
-            x[a, i] = held.tile([P, T], F32, name="x%d_%d" % (a, i))
+            x[a, i] = held.tile([P, T], F32, name="x%d_%d" % (a, i), align_bytes=256)
             rows = xT[512 * a : 512 * (a + 1), :].rearrange("(p i) t -> p i t", i=PACK)
             nc.sync.dma_start(out=x[a, i][:], in_=rows[:, i, :])
 
@@ -135,8 +135,8 @@ def tile_list_heads_tm_gelu_kernel(
             held.tile([P, S, PACK], BF16, name="grouped%d" % a, tag="grouped%d" % a, align_bytes=64)
             for a in range(PASSES)
         ]
-        codes = [held.tile([P, S], U32, name="codes%d" % a, align_bytes=64) for a in range(PASSES)]
-        planes = [held.tile([P, S], U8, name="planes%d" % a, align_bytes=64) for a in range(PASSES)]
+        codes = [held.tile([P, S], U32, name="codes%d" % a, align_bytes=256) for a in range(PASSES)]
+        planes = [held.tile([P, S], U8, name="planes%d" % a, align_bytes=256) for a in range(PASSES)]
 
         def gather(a, i, j0=0, j1=S):
             window = x[a, i][:].indirect(offsets[:, j0 // 16 : j1 // 16])

@@ -26,6 +26,8 @@ BANK = 512
 QUARTER = M // 4
 TILES = S // P
 QUAD_ROWS = 4
+SLOT = S + P
+EARLY = S - P
 
 
 def tile_list_heads_tm_gelu_kernel(
@@ -130,7 +132,9 @@ def tile_list_heads_tm_gelu_kernel(
                 in_=bank[:].rearrange("j (c p) -> j p c", c=4),
             )
 
-        picked = [held.tile([P, PACK, S], F32, name="picked%d" % a, align_bytes=64) for a in range(PASSES)]
+        picked = [held.tile([P, PACK, S], F32, name="picked%d" % a, align_bytes=64) for a in range(LAST)]
+        stairs = held.tile([P, PACK * SLOT], F32, name="stairs", align_bytes=64)
+        slots = stairs[:].rearrange("p (i c) -> p i c", i=PACK)
         grouped = [
             held.tile([P, S, PACK], BF16, name="grouped%d" % a, tag="grouped%d" % a, align_bytes=64)
             for a in range(PASSES)
@@ -138,23 +142,28 @@ def tile_list_heads_tm_gelu_kernel(
         codes = [held.tile([P, S], U32, name="codes%d" % a, align_bytes=256) for a in range(PASSES)]
         planes = [held.tile([P, S], U8, name="planes%d" % a, align_bytes=256) for a in range(PASSES)]
 
-        def gather(a, i, j0=0, j1=S):
+        def gather_into(picks, a, i, j0, j1):
             window = x[a, i][:].indirect(offsets[:, j0 // 16 : j1 // 16])
-            nc.vector.tensor_tensor(picked[a][:, i, j0:j1], window, factors[:, j0:j1], MULT)
+            nc.vector.tensor_tensor(picks, window, factors[:, j0:j1], MULT)
+
+        def gather(a, i, j0=0, j1=S):
+            gather_into(picked[a][:, i, j0:j1], a, i, j0, j1)
+
+        def interleave_from(picks, a, i, j0, j1):
+            nc.scalar.copy(
+                out=grouped[a][:, j0:j1, i].rearrange("p (c u) i -> p c i u", u=4),
+                in_=picks.rearrange("p i (c u) -> p c i u", u=4),
+            )
 
         def interleave(a, pair, j0=0, j1=S):
             i = slice(2 * pair, 2 * pair + 2)
-            nc.scalar.copy(
-                out=grouped[a][:, j0:j1, i].rearrange("p (c u) i -> p c i u", u=4),
-                in_=picked[a][:, i, j0:j1].rearrange("p i (c u) -> p c i u", u=4),
-            )
+            interleave_from(picked[a][:, i, j0:j1], a, i, j0, j1)
+
+        def quantize_from(values, a, j0, j1):
+            nc.vector.quantize_mx(out=codes[a][:, j0:j1].bitcast(FP8X4), scales=planes[a][:, j0:j1], in_=values)
 
         def quantize(a, j0, j1):
-            nc.vector.quantize_mx(
-                out=codes[a][:, j0:j1].bitcast(FP8X4),
-                scales=planes[a][:, j0:j1],
-                in_=grouped[a][:, j0:j1, :].rearrange("p j i -> p (j i)"),
-            )
+            quantize_from(grouped[a][:, j0:j1, :].rearrange("p j i -> p (j i)"), a, j0, j1)
 
         def multiply_w4(a, jt, h):
             j = slice(P * jt, P * (jt + 1))
@@ -199,39 +208,49 @@ def tile_list_heads_tm_gelu_kernel(
             if not in_halves:
                 nc.sync.dma_start(out=rows, in_=o[:])
 
-        def last_plane(jt):
-            gather(LAST, 3, P * jt, P * (jt + 1))
-            interleave(LAST, 1, P * jt, P * (jt + 1))
+        def close(jt, h):
+            multiply_w4(LAST, jt, h)
+            multiply_r8(LAST, jt, h)
 
-        for a in range(PASSES):
+        for a in range(LAST):
             gather(a, 0)
-            if a > 0:
-                quantize(a - 1, 0, S // 2)
-                quantize(a - 1, S // 2, S)
             if a == 1:
+                quantize(0, 0, S // 2)
+                quantize(0, S // 2, S)
                 sweep(multiply_w4, 0, (0, 1))
                 sweep(multiply_r8, 0, (0, 1))
-            if a == 2:
-                sweep(multiply_w4, 1, (0, 1))
-                sweep(multiply_r8, 1, (0, 1))
             gather(a, 1)
             interleave(a, 0)
             gather(a, 2)
-            if a < LAST:
-                for j0 in (0, S // 2):
-                    gather(a, 3, j0, j0 + S // 2)
-                    interleave(a, 1, j0, j0 + S // 2)
-        last_plane(0)
-        last_plane(1)
-        for jt in range(TILES):
+            for j0 in (0, S // 2):
+                gather(a, 3, j0, j0 + S // 2)
+                interleave(a, 1, j0, j0 + S // 2)
+
+        gather_into(slots[:, 0, 0:S], LAST, 0, 0, S)
+        quantize(1, 0, S // 2)
+        quantize(1, S // 2, S)
+        sweep(multiply_w4, 1, (0, 1))
+        sweep(multiply_r8, 1, (0, 1))
+        gather_into(slots[:, 1, 0:S], LAST, 1, 0, S)
+        interleave_from(slots[:, 0:2, 0:EARLY], LAST, slice(0, 2), 0, EARLY)
+        gather_into(slots[:, 2, 0:S], LAST, 2, 0, S)
+        for j0, j1 in ((0, P), (P, 2 * P), (2 * P, S)):
+            gather_into(slots[:, 3, j0:j1], LAST, 3, j0, j1)
+            interleave_from(slots[:, 2:4, j0 : j0 + P], LAST, slice(2, 4), j0, j0 + P)
+        quantize(LAST, 0, P)
+        close(0, 0)
+        final = stairs[:, 2 * SLOT - P : 2 * SLOT + P].bitcast(BF16)
+        nc.vector.tensor_copy(
+            out=final.rearrange("p (c u i) -> p c i u", u=4, i=PACK),
+            in_=slots[:, :, EARLY:S].rearrange("p i (c u) -> p c i u", u=4),
+        )
+        for jt in (1, 2):
             quantize(LAST, P * jt, P * (jt + 1))
-            multiply_w4(LAST, jt, 0)
-            multiply_r8(LAST, jt, 0)
-            if jt + 2 < TILES:
-                last_plane(jt + 2)
+            close(jt, 0)
+        quantize_from(final, LAST, EARLY, S)
+        close(3, 0)
         for jt in range(TILES):
-            multiply_w4(LAST, jt, 1)
-            multiply_r8(LAST, jt, 1)
+            close(jt, 1)
         for h in range(2):
             for jt in range(TILES):
                 finish(jt, h)

@@ -198,7 +198,7 @@ def tile_list_heads_tm_gelu_kernel(
         def finish(jt, h):
             y = stage.tile([P, BANK], F32, name="y")
             o = stage.tile([P, BANK], F32, name="o")
-            in_halves = (jt, h) in ((0, 0), (TILES - 1, 1))
+            in_halves = (jt, h) == (0, 0)
             rows = out[P * jt : P * (jt + 1), BANK * h : BANK * (h + 1)]
             for c in (slice(0, BANK // 2), slice(BANK // 2, BANK)):
                 nc.vector.tensor_tensor(y[:, c], banks[jt, h][:, c], bias[:, BANK * h : BANK * (h + 1)][:, c], ADD)

@@ -39,7 +39,7 @@ def tile_list_heads_tm_gelu_kernel(
         stage = ctx.enter_context(tc.tile_pool(name="stage", bufs=8))
         psum = ctx.enter_context(tc.psum_pool(name="psum", bufs=1))
 
-        factors = held.tile([P, S], F32, name="factors")
+        factors = held.tile([P, S], F32, name="factors", align_bytes=256)
         offsets = held.tile([P, S // 16], U16, name="offsets")
         b_cols = held.tile([P, M // P], F32, name="b_cols", tag="grouped0", align_bytes=64)
         nc.sync.dma_start(factors[:], wgt)
@@ -197,7 +197,7 @@ def tile_list_heads_tm_gelu_kernel(
 
         def finish(jt, h):
             y = stage.tile([P, BANK], F32, name="y")
-            o = stage.tile([P, BANK], F32, name="o")
+            o = stage.tile([P, BANK], F32, name="o", align_bytes=256)
             in_halves = (jt, h) == (0, 0)
             rows = out[P * jt : P * (jt + 1), BANK * h : BANK * (h + 1)]
             for c in (slice(0, BANK // 2), slice(BANK // 2, BANK)):

@@ -206,7 +206,8 @@ def tile_list_heads_tm_gelu_kernel(
                 if in_halves:
                     nc.sync.dma_start(out=rows[:, c], in_=o[:, c])
             if not in_halves:
-                nc.sync.dma_start(out=rows, in_=o[:])
+                queue = nc.scalar if (jt, h) == (TILES - 1, 1) else nc.sync
+                queue.dma_start(out=rows, in_=o[:])
 
         def close(jt, h):
             multiply_w4(LAST, jt, h)

from contextlib import ExitStack

import concourse.mybir as mybir
from concourse.masks import make_identity

K, M, T, S = 1536, 1024, 1024, 512
FLOPS = 2 * 2 * K * M * S

F32 = mybir.dt.float32
BF16 = mybir.dt.bfloat16
I32 = mybir.dt.int32
U32 = mybir.dt.uint32
U16 = mybir.dt.uint16
U8 = mybir.dt.uint8
FP8X4 = mybir.dt.float8_e4m3fn_x4
FP4X4 = mybir.dt.float4_e2m1fn_x4
ADD = mybir.AluOpType.add
MULT = mybir.AluOpType.mult
GELU = mybir.ActivationFunctionType.Gelu_apprx_tanh

P = 128
PACK = 4
PASSES = K // (P * PACK)
LAST = PASSES - 1
BANK = 512
QUARTER = M // 4
TILES = S // P
QUAD_ROWS = 4
SLOT = S + P
EARLY = S - P


def tile_list_heads_tm_gelu_kernel(
    tc, xT, w4_words, w4_scales, r8_words, r8_scales, wgt, b, offs, out
):
    nc = tc.nc
    with ExitStack() as ctx:
        held = ctx.enter_context(tc.tile_pool(name="held", bufs=1))
        stage = ctx.enter_context(tc.tile_pool(name="stage", bufs=8))
        psum = ctx.enter_context(tc.psum_pool(name="psum", bufs=1))

        factors = held.tile([P, S], F32, name="factors", align_bytes=256)
        offsets = held.tile([P, S // 16], U16, name="offsets")
        b_cols = held.tile([P, M // P], F32, name="b_cols", tag="grouped0", align_bytes=64)
        nc.sync.dma_start(factors[:], wgt)
        nc.sync.dma_start(offsets[:], offs)
        nc.scalar.dma_start(out=b_cols[:], in_=b.rearrange("(p c) -> p c", c=M // P))

        w4_planes = held.tile([P, PASSES, M], U8, name="w4_planes", align_bytes=256)
        r8_planes = held.tile([P, M], U8, name="r8_planes", align_bytes=256)
        nc.vector.memset(r8_planes[:].bitcast(I32), 0)
        nc.vector.memset(w4_planes[:].bitcast(I32), 0)

        warm = held.tile([P, 1], F32, name="warm")
        nc.vector.memset(warm[:], 0.0)
        nc.scalar.activation(warm[:], warm[:], GELU)

        for q in range(4):
            nc.gpsimd.dma_start(
                out=r8_planes[32 * q + QUAD_ROWS : 32 * q + QUAD_ROWS * (PASSES + 1), :].bitcast(I32),
                in_=r8_scales[:, 4 * q : 4 * q + 4, :].bitcast(I32),
            )
        ident = held.tile([P, P], F32, name="ident")
        make_identity(nc, ident[:])

        x = {}
        w4 = [held.tile([P, 2 * M], U8, name="w4_%d" % a, align_bytes=256) for a in range(PASSES)]
        r8 = [held.tile([P, M], U32, name="r8_%d" % a, align_bytes=256) for a in range(PASSES)]

        def load_plane(a, i):
            x[a, i] = held.tile([P, T], F32, name="x%d_%d" % (a, i), align_bytes=256)
            rows = xT[512 * a : 512 * (a + 1), :].rearrange("(p i) t -> p i t", i=PACK)
            nc.sync.dma_start(out=x[a, i][:], in_=rows[:, i, :])

        def load_w4_scales(r):
            nc.sync.dma_start(
                out=w4_planes[r:P:32, :, :].bitcast(I32),
                in_=w4_scales[:, r:16:4, :].rearrange("a q n -> q a n").bitcast(I32),
            )

        def load_w4(a, n0, n1):
            nc.sync.dma_start(
                out=w4[a][:, 2 * n0 : 2 * n1].bitcast(I32), in_=w4_words[a][:, 2 * n0 : 2 * n1].bitcast(I32)
            )

        def load_r8(a, n0, n1):
            nc.sync.dma_start(
                out=r8[a][:, n0:n1].bitcast(I32),
                in_=r8_words[a].rearrange("p n t -> p (n t)")[:, 4 * n0 : 4 * n1].bitcast(I32),
            )

        load_plane(0, 0)
        load_plane(0, 1)
        load_w4_scales(0)
        load_plane(0, 2)
        load_w4_scales(1)
        load_plane(0, 3)
        load_plane(1, 0)
        load_w4_scales(2)
        load_plane(1, 1)
        load_w4_scales(3)
        load_w4(0, 0, M)
        load_plane(1, 2)
        load_r8(0, 0, BANK)
        load_plane(1, 3)
        load_plane(2, 0)
        load_r8(0, BANK, M)
        load_w4(1, 0, M)
        load_plane(2, 1)
        load_plane(2, 2)
        load_r8(1, 0, BANK)
        load_plane(2, 3)
        load_r8(1, BANK, M)
        load_w4(2, 0, BANK)
        load_r8(2, 0, BANK)
        load_w4(2, BANK, M)
        load_r8(2, BANK, M)

        banks = {}
        for h in range(2):
            for jt in range(TILES):
                banks[jt, h] = psum.tile([P, BANK], F32, name="bank%d_%d" % (jt, h))

        bias = held.tile([P, M], F32, name="bias")
        for g in range(2):
            bank = banks[TILES - 1, g]
            for c in range(4):
                column = b_cols[:, 4 * g + c : 4 * g + c + 1]
                nc.tensor.transpose(bank[:, P * c : P * (c + 1)], column.to_broadcast([P, P]), ident[:])
            nc.scalar.copy(
                out=bias[:].rearrange("j (p c) -> j p c", c=8)[:, :, 4 * g : 4 * g + 4],
                in_=bank[:].rearrange("j (c p) -> j p c", c=4),
            )

        picked = [held.tile([P, PACK, S], F32, name="picked%d" % a, align_bytes=64) for a in range(LAST)]
        stairs = held.tile([P, PACK * SLOT], F32, name="stairs", align_bytes=64)
        slots = stairs[:].rearrange("p (i c) -> p i c", i=PACK)
        grouped = [
            held.tile([P, S, PACK], BF16, name="grouped%d" % a, tag="grouped%d" % a, align_bytes=64)
            for a in range(PASSES)
        ]
        codes = [held.tile([P, S], U32, name="codes%d" % a, align_bytes=256) for a in range(PASSES)]
        planes = [held.tile([P, S], U8, name="planes%d" % a, align_bytes=256) for a in range(PASSES)]

        def gather_into(picks, a, i, j0, j1):
            window = x[a, i][:].indirect(offsets[:, j0 // 16 : j1 // 16])
            nc.vector.tensor_tensor(picks, window, factors[:, j0:j1], MULT)

        def gather(a, i, j0=0, j1=S):
            gather_into(picked[a][:, i, j0:j1], a, i, j0, j1)

        def interleave_from(picks, a, i, j0, j1):
            nc.scalar.copy(
                out=grouped[a][:, j0:j1, i].rearrange("p (c u) i -> p c i u", u=4),
                in_=picks.rearrange("p i (c u) -> p c i u", u=4),
            )

        def interleave(a, pair, j0=0, j1=S):
            i = slice(2 * pair, 2 * pair + 2)
            interleave_from(picked[a][:, i, j0:j1], a, i, j0, j1)

        def quantize_from(values, a, j0, j1):
            nc.vector.quantize_mx(out=codes[a][:, j0:j1].bitcast(FP8X4), scales=planes[a][:, j0:j1], in_=values)

        def quantize(a, j0, j1):
            quantize_from(grouped[a][:, j0:j1, :].rearrange("p j i -> p (j i)"), a, j0, j1)

        def multiply_w4(a, jt, h):
            j = slice(P * jt, P * (jt + 1))
            nc.tensor.matmul_mx(
                out=banks[jt, h][:],
                lhsT=codes[a][:, j].bitcast(FP8X4),
                lhsT_scale=planes[a][:, j],
                rhs=w4[a][:, 2 * BANK * h : 2 * BANK * (h + 1)].bitcast(FP4X4),
                rhs_scale=w4_planes[:, a, BANK * h : BANK * (h + 1)],
                start=(a == 0),
                stop=False,
            )

        def multiply_r8(a, jt, h, c0=0, c1=BANK):
            j = slice(P * jt, P * (jt + 1))
            n = slice(BANK * h + c0, BANK * h + c1)
            nc.tensor.matmul_mx(
                out=banks[jt, h][:, c0:c1],
                lhsT=codes[a][:, j].bitcast(FP8X4),
                lhsT_scale=planes[a][:, j],
                rhs=r8[a][:, n].bitcast(FP8X4),
                rhs_scale=r8_planes[QUAD_ROWS * (a + 1) : P, n],
                start=False,
                stop=(a == LAST),
            )

        def sweep(multiply, a, halves):
            for h in halves:
                for jt in range(TILES):
                    multiply(a, jt, h)

        def finish(jt, h):
            y = stage.tile([P, BANK], F32, name="y")
            o = stage.tile([P, BANK], F32, name="o", align_bytes=256)
            in_halves = (jt, h) == (0, 0)
            rows = out[P * jt : P * (jt + 1), BANK * h : BANK * (h + 1)]
            for c in (slice(0, BANK // 2), slice(BANK // 2, BANK)):
                nc.vector.tensor_tensor(y[:, c], banks[jt, h][:, c], bias[:, BANK * h : BANK * (h + 1)][:, c], ADD)
                nc.scalar.activation(o[:, c], y[:, c], GELU)
                if in_halves:
                    nc.sync.dma_start(out=rows[:, c], in_=o[:, c])
            if not in_halves:
                queue = nc.scalar if (jt, h) == (TILES - 1, 1) else nc.sync
                queue.dma_start(out=rows, in_=o[:])

        def close(jt, h):
            multiply_w4(LAST, jt, h)
            multiply_r8(LAST, jt, h)

        for a in range(LAST):
            gather(a, 0)
            if a == 1:
                quantize(0, 0, S // 2)
                quantize(0, S // 2, S)
                sweep(multiply_w4, 0, (0, 1))
                sweep(multiply_r8, 0, (0, 1))
            gather(a, 1)
            interleave(a, 0)
            gather(a, 2)
            for j0 in (0, S // 2):
                gather(a, 3, j0, j0 + S // 2)
                interleave(a, 1, j0, j0 + S // 2)

        gather_into(slots[:, 0, 0:S], LAST, 0, 0, S)
        quantize(1, 0, S // 2)
        quantize(1, S // 2, S)
        sweep(multiply_w4, 1, (0, 1))
        sweep(multiply_r8, 1, (0, 1))
        gather_into(slots[:, 1, 0:S], LAST, 1, 0, S)
        interleave_from(slots[:, 0:2, 0:EARLY], LAST, slice(0, 2), 0, EARLY)
        gather_into(slots[:, 2, 0:S], LAST, 2, 0, S)
        for j0, j1 in ((0, P), (P, 2 * P), (2 * P, S)):
            gather_into(slots[:, 3, j0:j1], LAST, 3, j0, j1)
            interleave_from(slots[:, 2:4, j0 : j0 + P], LAST, slice(2, 4), j0, j0 + P)
        quantize(LAST, 0, P)
        close(0, 0)
        final = stairs[:, 2 * SLOT - P : 2 * SLOT + P].bitcast(BF16)
        nc.vector.tensor_copy(
            out=final.rearrange("p (c u i) -> p c i u", u=4, i=PACK),
            in_=slots[:, :, EARLY:S].rearrange("p i (c u) -> p c i u", u=4),
        )
        for jt in (1, 2):
            quantize(LAST, P * jt, P * (jt + 1))
            close(jt, 0)
        quantize_from(final, LAST, EARLY, S)
        close(3, 0)
        for jt in range(TILES):
            close(jt, 1)
        for h in range(2):
            for jt in range(TILES):
                finish(jt, h)
